import numpy as np
import ml_dtypes

BF16 = ml_dtypes.bfloat16


def bf(x):
    return np.asarray(x, np.float32).astype(BF16)


def f32(x):
    return np.asarray(x, np.float32)


def f64(x):
    return np.asarray(x).astype(np.float64)


def striped(idx):
    return np.tile(idx.reshape(-1, 16).T, (8, 1))


S, K, M, N, D, V = 1024, 128, 512, 768, 3, 256


def setup_inputs():
    return {"table": bf(np.random.standard_normal((K, S))), "w": bf(np.random.standard_normal((D, K, M)) / np.sqrt(D * K)), "c": f32(0.2 + 0.8 * np.random.random_sample((1, V))), "offs": striped(np.random.permutation(np.tile(np.arange(S), 2))[:N])}


def reference(table, w, c, offs):
    idx = offs[:16].T.reshape(-1)
    x = f64(table)[:, idx]
    y = sum(f64(w)[t].T @ x[:, t * V : (t + 1) * V] for t in range(D))
    return y * f64(c)

@@ -1,0 +1,47 @@
+import concourse.mybir as mybir
+
+BF16, F32, U16 = mybir.dt.bfloat16, mybir.dt.float32, mybir.dt.uint16
+
+P = 128
+NODES = 1024
+RELATIONS = 3
+PICKED = 256
+FEATURES = 512
+BLOCKS = FEATURES // P
+PIECE_COLUMNS = PICKED // 16
+
+FLOPS = 2 * RELATIONS * P * FEATURES * PICKED
+
+
+def tile_gather_matmul_kernel(tc, table, w, c, offs, out):
+    nc = tc.nc
+    with (
+        tc.tile_pool(name="held", bufs=1) as held,
+        tc.psum_pool(name="banks", bufs=1) as banks,
+    ):
+        offsets = held.tile([P, RELATIONS * PIECE_COLUMNS], U16, name="offsets")
+        nodes = held.tile([P, NODES], BF16, name="nodes")
+        weights = held.tile([P, RELATIONS, FEATURES], BF16, name="weights")
+        factor = held.tile([P, PICKED], F32, name="factor")
+        scaled = held.tile([P, BLOCKS, PICKED], F32, name="scaled")
+
+        nc.sync.dma_start(offsets[:], offs)
+        nc.scalar.dma_start(nodes[:], table)
+        nc.sync.dma_start(weights[:], w.rearrange("t k m -> k t m"))
+        nc.gpsimd.dma_start(factor[:], c.rearrange("o v -> (o v)").partition_broadcast(P))
+
+        out_blocks = out.rearrange("(b p) v -> b p v", p=P)
+        for b in range(BLOCKS):
+            bank = banks.tile([P, PICKED], F32, name=f"bank{b}")
+            for t in range(RELATIONS):
+                picked = nodes[:].indirect(offsets[:, t * PIECE_COLUMNS : (t + 1) * PIECE_COLUMNS])
+                nc.tensor.matmul(
+                    bank[:],
+                    weights[:, t, b * P : (b + 1) * P],
+                    picked,
+                    start=(t == 0),
+                    stop=(t == RELATIONS - 1),
+                )
+            nc.vector.tensor_tensor(scaled[:, b, :], bank[:], factor[:], mybir.AluOpType.mult)
+            queue = nc.sync if b % 2 == 0 else nc.scalar
+            queue.dma_start(out_blocks[b], scaled[:, b, :])

@@ -21,27 +21,42 @@ def tile_gather_matmul_kernel(tc, table, w, c, offs, out):
     ):
         offsets = held.tile([P, RELATIONS * PIECE_COLUMNS], U16, name="offsets")
         nodes = held.tile([P, NODES], BF16, name="nodes")
-        weights = held.tile([P, RELATIONS, FEATURES], BF16, name="weights")
+        weights = [held.tile([P, FEATURES], BF16, name=f"weights{t}") for t in range(RELATIONS)]
+        c_row = held.tile([1, PICKED], F32, name="c_row")
+        ones = held.tile([1, P], F32, name="ones")
         factor = held.tile([P, PICKED], F32, name="factor")
         scaled = held.tile([P, BLOCKS, PICKED], F32, name="scaled")
 
         nc.sync.dma_start(offsets[:], offs)
+        nc.scalar.dma_start(c_row[:], c)
+        nc.sync.dma_start(weights[0][:], w[0])
         nc.scalar.dma_start(nodes[:], table)
-        nc.sync.dma_start(weights[:], w.rearrange("t k m -> k t m"))
-        nc.gpsimd.dma_start(factor[:], c.rearrange("o v -> (o v)").partition_broadcast(P))
+        nc.scalar.dma_start(weights[1][:], w[1])
+        nc.scalar.dma_start(weights[2][:], w[2])
+
+        nc.vector.memset(ones[:], 1.0)
+        c_bank = banks.tile([P, PICKED], F32, name="c_bank")
+        nc.tensor.matmul(c_bank[:], ones[:], c_row[:], start=True, stop=True)
+        nc.vector.tensor_copy(factor[:], c_bank[:])
+
+        def product(bank, b, t):
+            picked = nodes[:].indirect(offsets[:, t * PIECE_COLUMNS : (t + 1) * PIECE_COLUMNS])
+            nc.tensor.matmul(
+                bank[:],
+                weights[t][:, b * P : (b + 1) * P],
+                picked,
+                start=(t == 0),
+                stop=(t == RELATIONS - 1),
+            )
+
+        sums = [banks.tile([P, PICKED], F32, name=f"sum{b}") for b in range(BLOCKS)]
+        for b in range(BLOCKS):
+            product(sums[b], b, 0)
 
         out_blocks = out.rearrange("(b p) v -> b p v", p=P)
         for b in range(BLOCKS):
-            bank = banks.tile([P, PICKED], F32, name=f"bank{b}")
-            for t in range(RELATIONS):
-                picked = nodes[:].indirect(offsets[:, t * PIECE_COLUMNS : (t + 1) * PIECE_COLUMNS])
-                nc.tensor.matmul(
-                    bank[:],
-                    weights[:, t, b * P : (b + 1) * P],
-                    picked,
-                    start=(t == 0),
-                    stop=(t == RELATIONS - 1),
-                )
-            nc.vector.tensor_tensor(scaled[:, b, :], bank[:], factor[:], mybir.AluOpType.mult)
+            for t in range(1, RELATIONS):
+                product(sums[b], b, t)
+            nc.vector.tensor_tensor(scaled[:, b, :], sums[b][:], factor[:], mybir.AluOpType.mult)
             queue = nc.sync if b % 2 == 0 else nc.scalar
             queue.dma_start(out_blocks[b], scaled[:, b, :])

@@ -29,8 +29,9 @@ def tile_gather_matmul_kernel(tc, table, w, c, offs, out):
 
         nc.sync.dma_start(offsets[:], offs)
         nc.scalar.dma_start(c_row[:], c)
-        nc.sync.dma_start(weights[0][:], w[0])
+        nc.sync.dma_start(weights[0][:, 0:P], w[0][:, 0:P])
         nc.scalar.dma_start(nodes[:], table)
+        nc.scalar.dma_start(weights[0][:, P:FEATURES], w[0][:, P:FEATURES])
         nc.scalar.dma_start(weights[1][:], w[1])
         nc.scalar.dma_start(weights[2][:], w[2])
 

@@ -9,6 +9,7 @@ PICKED = 256
 FEATURES = 512
 BLOCKS = FEATURES // P
 PIECE_COLUMNS = PICKED // 16
+SQUARE = 32
 
 FLOPS = 2 * RELATIONS * P * FEATURES * PICKED
 
@@ -22,23 +23,27 @@ def tile_gather_matmul_kernel(tc, table, w, c, offs, out):
         offsets = held.tile([P, RELATIONS * PIECE_COLUMNS], U16, name="offsets")
         nodes = held.tile([P, NODES], BF16, name="nodes")
         weights = [held.tile([P, FEATURES], BF16, name=f"weights{t}") for t in range(RELATIONS)]
-        c_row = held.tile([1, PICKED], F32, name="c_row")
-        ones = held.tile([1, P], F32, name="ones")
-        factor = held.tile([P, PICKED], F32, name="factor")
+        c_rows = held.tile([P, PICKED], F32, name="c_rows", align_bytes=64)
+        c_columns = held.tile([P, PICKED], F32, name="c_columns", align_bytes=64)
+        c_repeated = held.tile([P, PICKED], F32, name="c_repeated", align_bytes=64)
+        factor = held.tile([P, PICKED], F32, name="factor", align_bytes=64)
         scaled = held.tile([P, BLOCKS, PICKED], F32, name="scaled")
 
+        nc.vector.memset(c_rows[:], 0.0)
         nc.sync.dma_start(offsets[:], offs)
-        nc.scalar.dma_start(c_row[:], c)
         nc.sync.dma_start(weights[0][:, 0:P], w[0][:, 0:P])
+        nc.sync.dma_start(c_rows[0:P:SQUARE, :], c.rearrange("o v -> (o v)").partition_broadcast(P // SQUARE))
         nc.scalar.dma_start(nodes[:], table)
         nc.scalar.dma_start(weights[0][:, P:FEATURES], w[0][:, P:FEATURES])
         nc.scalar.dma_start(weights[1][:], w[1])
         nc.scalar.dma_start(weights[2][:], w[2])
 
-        nc.vector.memset(ones[:], 1.0)
-        c_bank = banks.tile([P, PICKED], F32, name="c_bank")
-        nc.tensor.matmul(c_bank[:], ones[:], c_row[:], start=True, stop=True)
-        nc.vector.tensor_copy(factor[:], c_bank[:])
+        nc.vector.transpose(c_columns[:], c_rows[:])
+        nc.vector.tensor_copy(
+            c_repeated[:].rearrange("p (s q) -> p s q", q=SQUARE),
+            c_columns[:].rearrange("p (s q) -> p s q", q=SQUARE)[:, :, 0:1].to_broadcast([P, PICKED // SQUARE, SQUARE]),
+        )
+        nc.vector.transpose(factor[:], c_repeated[:])
 
         def product(bank, b, t):
             picked = nodes[:].indirect(offsets[:, t * PIECE_COLUMNS : (t + 1) * PIECE_COLUMNS])

@@ -10,6 +10,7 @@ FEATURES = 512
 BLOCKS = FEATURES // P
 PIECE_COLUMNS = PICKED // 16
 SQUARE = 32
+PAIR = 2
 
 FLOPS = 2 * RELATIONS * P * FEATURES * PICKED
 
@@ -22,7 +23,10 @@ def tile_gather_matmul_kernel(tc, table, w, c, offs, out):
     ):
         offsets = held.tile([P, RELATIONS * PIECE_COLUMNS], U16, name="offsets")
         nodes = held.tile([P, NODES], BF16, name="nodes")
-        weights = [held.tile([P, FEATURES], BF16, name=f"weights{t}") for t in range(RELATIONS)]
+        first_weights = held.tile([P, FEATURES], BF16, name="first_weights")
+        later_weights = [
+            held.tile([P, RELATIONS - 1, PAIR * P], BF16, name=f"later_weights{pair}") for pair in range(BLOCKS // PAIR)
+        ]
         c_rows = held.tile([P, PICKED], F32, name="c_rows", align_bytes=64)
         c_columns = held.tile([P, PICKED], F32, name="c_columns", align_bytes=64)
         c_repeated = held.tile([P, PICKED], F32, name="c_repeated", align_bytes=64)
@@ -31,12 +35,13 @@ def tile_gather_matmul_kernel(tc, table, w, c, offs, out):
 
         nc.vector.memset(c_rows[:], 0.0)
         nc.sync.dma_start(offsets[:], offs)
-        nc.sync.dma_start(weights[0][:, 0:P], w[0][:, 0:P])
+        nc.sync.dma_start(first_weights[:, 0:P], w[0][:, 0:P])
         nc.sync.dma_start(c_rows[0:P:SQUARE, :], c.rearrange("o v -> (o v)").partition_broadcast(P // SQUARE))
         nc.scalar.dma_start(nodes[:], table)
-        nc.scalar.dma_start(weights[0][:, P:FEATURES], w[0][:, P:FEATURES])
-        nc.scalar.dma_start(weights[1][:], w[1])
-        nc.scalar.dma_start(weights[2][:], w[2])
+        nc.scalar.dma_start(first_weights[:, P:FEATURES], w[0][:, P:FEATURES])
+        for pair in range(BLOCKS // PAIR):
+            columns = slice(pair * PAIR * P, (pair + 1) * PAIR * P)
+            nc.scalar.dma_start(later_weights[pair][:], w[1:RELATIONS, :, columns].rearrange("t k m -> k t m"))
 
         nc.vector.transpose(c_columns[:], c_rows[:])
         nc.vector.tensor_copy(
@@ -45,11 +50,17 @@ def tile_gather_matmul_kernel(tc, table, w, c, offs, out):
         )
         nc.vector.transpose(factor[:], c_repeated[:])
 
+        def block_weights(b, t):
+            if t == 0:
+                return first_weights[:, b * P : (b + 1) * P]
+            pair, place = divmod(b, PAIR)
+            return later_weights[pair][:, t - 1, place * P : (place + 1) * P]
+
         def product(bank, b, t):
             picked = nodes[:].indirect(offsets[:, t * PIECE_COLUMNS : (t + 1) * PIECE_COLUMNS])
             nc.tensor.matmul(
                 bank[:],
-                weights[t][:, b * P : (b + 1) * P],
+                block_weights(b, t),
                 picked,
                 start=(t == 0),
                 stop=(t == RELATIONS - 1),

@@ -36,8 +36,8 @@ def tile_gather_matmul_kernel(tc, table, w, c, offs, out):
         nc.vector.memset(c_rows[:], 0.0)
         nc.sync.dma_start(offsets[:], offs)
         nc.sync.dma_start(first_weights[:, 0:P], w[0][:, 0:P])
-        nc.sync.dma_start(c_rows[0:P:SQUARE, :], c.rearrange("o v -> (o v)").partition_broadcast(P // SQUARE))
         nc.scalar.dma_start(nodes[:], table)
+        nc.scalar.dma_start(c_rows[0:P:SQUARE, :], c.rearrange("o v -> (o v)").partition_broadcast(P // SQUARE))
         nc.scalar.dma_start(first_weights[:, P:FEATURES], w[0][:, P:FEATURES])
         for pair in range(BLOCKS // PAIR):
             columns = slice(pair * PAIR * P, (pair + 1) * PAIR * P)

@@ -10,7 +10,6 @@ FEATURES = 512
 BLOCKS = FEATURES // P
 PIECE_COLUMNS = PICKED // 16
 SQUARE = 32
-PAIR = 2
 
 FLOPS = 2 * RELATIONS * P * FEATURES * PICKED
 
@@ -23,10 +22,7 @@ def tile_gather_matmul_kernel(tc, table, w, c, offs, out):
     ):
         offsets = held.tile([P, RELATIONS * PIECE_COLUMNS], U16, name="offsets")
         nodes = held.tile([P, NODES], BF16, name="nodes")
-        first_weights = held.tile([P, FEATURES], BF16, name="first_weights")
-        later_weights = [
-            held.tile([P, RELATIONS - 1, PAIR * P], BF16, name=f"later_weights{pair}") for pair in range(BLOCKS // PAIR)
-        ]
+        weights = [held.tile([P, FEATURES], BF16, name=f"weights{t}") for t in range(RELATIONS)]
         c_rows = held.tile([P, PICKED], F32, name="c_rows", align_bytes=64)
         c_columns = held.tile([P, PICKED], F32, name="c_columns", align_bytes=64)
         c_repeated = held.tile([P, PICKED], F32, name="c_repeated", align_bytes=64)
@@ -35,13 +31,12 @@ def tile_gather_matmul_kernel(tc, table, w, c, offs, out):
 
         nc.vector.memset(c_rows[:], 0.0)
         nc.sync.dma_start(offsets[:], offs)
-        nc.sync.dma_start(first_weights[:, 0:P], w[0][:, 0:P])
+        nc.sync.dma_start(weights[0][:, 0:P], w[0][:, 0:P])
         nc.scalar.dma_start(nodes[:], table)
         nc.scalar.dma_start(c_rows[0:P:SQUARE, :], c.rearrange("o v -> (o v)").partition_broadcast(P // SQUARE))
-        nc.scalar.dma_start(first_weights[:, P:FEATURES], w[0][:, P:FEATURES])
-        for pair in range(BLOCKS // PAIR):
-            columns = slice(pair * PAIR * P, (pair + 1) * PAIR * P)
-            nc.scalar.dma_start(later_weights[pair][:], w[1:RELATIONS, :, columns].rearrange("t k m -> k t m"))
+        nc.scalar.dma_start(weights[0][:, P:FEATURES], w[0][:, P:FEATURES])
+        nc.scalar.dma_start(weights[1][:], w[1])
+        nc.scalar.dma_start(weights[2][:], w[2])
 
         nc.vector.transpose(c_columns[:], c_rows[:])
         nc.vector.tensor_copy(
@@ -50,30 +45,19 @@ def tile_gather_matmul_kernel(tc, table, w, c, offs, out):
         )
         nc.vector.transpose(factor[:], c_repeated[:])
 
-        def block_weights(b, t):
-            if t == 0:
-                return first_weights[:, b * P : (b + 1) * P]
-            pair, place = divmod(b, PAIR)
-            return later_weights[pair][:, t - 1, place * P : (place + 1) * P]
-
-        def product(bank, b, t):
+        def product(bank, b, t, first, last):
             picked = nodes[:].indirect(offsets[:, t * PIECE_COLUMNS : (t + 1) * PIECE_COLUMNS])
-            nc.tensor.matmul(
-                bank[:],
-                block_weights(b, t),
-                picked,
-                start=(t == 0),
-                stop=(t == RELATIONS - 1),
-            )
+            nc.tensor.matmul(bank[:], weights[t][:, b * P : (b + 1) * P], picked, start=first, stop=last)
 
         sums = [banks.tile([P, PICKED], F32, name=f"sum{b}") for b in range(BLOCKS)]
         for b in range(BLOCKS):
-            product(sums[b], b, 0)
+            product(sums[b], b, 0, first=True, last=False)
 
         out_blocks = out.rearrange("(b p) v -> b p v", p=P)
         for b in range(BLOCKS):
-            for t in range(1, RELATIONS):
-                product(sums[b], b, t)
+            second, third = (1, 2) if b < BLOCKS // 2 else (2, 1)
+            product(sums[b], b, second, first=False, last=False)
+            product(sums[b], b, third, first=False, last=True)
             nc.vector.tensor_tensor(scaled[:, b, :], sums[b][:], factor[:], mybir.AluOpType.mult)
             queue = nc.sync if b % 2 == 0 else nc.scalar
             queue.dma_start(out_blocks[b], scaled[:, b, :])

@@ -59,5 +59,5 @@ def tile_gather_matmul_kernel(tc, table, w, c, offs, out):
             product(sums[b], b, second, first=False, last=False)
             product(sums[b], b, third, first=False, last=True)
             nc.vector.tensor_tensor(scaled[:, b, :], sums[b][:], factor[:], mybir.AluOpType.mult)
-            queue = nc.sync if b % 2 == 0 else nc.scalar
-            queue.dma_start(out_blocks[b], scaled[:, b, :])
+            for queue, rows in ((nc.sync, slice(0, P // 2)), (nc.scalar, slice(P // 2, P))):
+                queue.dma_start(out_blocks[b][rows, :], scaled[rows, b, :])

@@ -58,6 +58,13 @@ def tile_gather_matmul_kernel(tc, table, w, c, offs, out):
             second, third = (1, 2) if b < BLOCKS // 2 else (2, 1)
             product(sums[b], b, second, first=False, last=False)
             product(sums[b], b, third, first=False, last=True)
-            nc.vector.tensor_tensor(scaled[:, b, :], sums[b][:], factor[:], mybir.AluOpType.mult)
-            for queue, rows in ((nc.sync, slice(0, P // 2)), (nc.scalar, slice(P // 2, P))):
-                queue.dma_start(out_blocks[b][rows, :], scaled[rows, b, :])
+            if b < BLOCKS - 1:
+                nc.vector.tensor_tensor(scaled[:, b, :], sums[b][:], factor[:], mybir.AluOpType.mult)
+                for queue, rows in ((nc.sync, slice(0, P // 2)), (nc.scalar, slice(P // 2, P))):
+                    queue.dma_start(out_blocks[b][rows, :], scaled[rows, b, :])
+            else:
+                for queue, columns in ((nc.sync, slice(0, PICKED // 2)), (nc.scalar, slice(PICKED // 2, PICKED))):
+                    nc.vector.tensor_tensor(
+                        scaled[:, b, columns], sums[b][:, columns], factor[:, columns], mybir.AluOpType.mult
+                    )
+                    queue.dma_start(out_blocks[b][:, columns], scaled[:, b, columns])

@@ -58,13 +58,8 @@ def tile_gather_matmul_kernel(tc, table, w, c, offs, out):
             second, third = (1, 2) if b < BLOCKS // 2 else (2, 1)
             product(sums[b], b, second, first=False, last=False)
             product(sums[b], b, third, first=False, last=True)
-            if b < BLOCKS - 1:
-                nc.vector.tensor_tensor(scaled[:, b, :], sums[b][:], factor[:], mybir.AluOpType.mult)
-                for queue, rows in ((nc.sync, slice(0, P // 2)), (nc.scalar, slice(P // 2, P))):
-                    queue.dma_start(out_blocks[b][rows, :], scaled[rows, b, :])
-            else:
-                for queue, columns in ((nc.sync, slice(0, PICKED // 2)), (nc.scalar, slice(PICKED // 2, PICKED))):
-                    nc.vector.tensor_tensor(
-                        scaled[:, b, columns], sums[b][:, columns], factor[:, columns], mybir.AluOpType.mult
-                    )
-                    queue.dma_start(out_blocks[b][:, columns], scaled[:, b, columns])
+            for queue, columns in ((nc.sync, slice(0, PICKED // 2)), (nc.scalar, slice(PICKED // 2, PICKED))):
+                nc.vector.tensor_tensor(
+                    scaled[:, b, columns], sums[b][:, columns], factor[:, columns], mybir.AluOpType.mult
+                )
+                queue.dma_start(out_blocks[b][:, columns], scaled[:, b, columns])

@@ -9,6 +9,7 @@ PICKED = 256
 FEATURES = 512
 BLOCKS = FEATURES // P
 PIECE_COLUMNS = PICKED // 16
+PAIR = 2 * P
 SQUARE = 32
 
 FLOPS = 2 * RELATIONS * P * FEATURES * PICKED
@@ -22,7 +23,10 @@ def tile_gather_matmul_kernel(tc, table, w, c, offs, out):
     ):
         offsets = held.tile([P, RELATIONS * PIECE_COLUMNS], U16, name="offsets")
         nodes = held.tile([P, NODES], BF16, name="nodes")
-        weights = [held.tile([P, FEATURES], BF16, name=f"weights{t}") for t in range(RELATIONS)]
+        first_weights = held.tile([P, FEATURES], BF16, name="first_weights")
+        later_weights = [
+            held.tile([P, RELATIONS - 1, PAIR], BF16, name=f"later_weights{h}") for h in range(FEATURES // PAIR)
+        ]
         c_rows = held.tile([P, PICKED], F32, name="c_rows", align_bytes=64)
         c_columns = held.tile([P, PICKED], F32, name="c_columns", align_bytes=64)
         c_repeated = held.tile([P, PICKED], F32, name="c_repeated", align_bytes=64)
@@ -31,12 +35,14 @@ def tile_gather_matmul_kernel(tc, table, w, c, offs, out):
 
         nc.vector.memset(c_rows[:], 0.0)
         nc.sync.dma_start(offsets[:], offs)
-        nc.sync.dma_start(weights[0][:, 0:P], w[0][:, 0:P])
+        nc.sync.dma_start(first_weights[:, 0:P], w[0][:, 0:P])
         nc.scalar.dma_start(nodes[:], table)
         nc.scalar.dma_start(c_rows[0:P:SQUARE, :], c.rearrange("o v -> (o v)").partition_broadcast(P // SQUARE))
-        nc.scalar.dma_start(weights[0][:, P:FEATURES], w[0][:, P:FEATURES])
-        nc.scalar.dma_start(weights[1][:], w[1])
-        nc.scalar.dma_start(weights[2][:], w[2])
+        nc.scalar.dma_start(first_weights[:, P:FEATURES], w[0][:, P:FEATURES])
+        for h in range(FEATURES // PAIR):
+            nc.scalar.dma_start(
+                later_weights[h][:], w[1:RELATIONS, :, h * PAIR : (h + 1) * PAIR].rearrange("t k m -> k t m")
+            )
 
         nc.vector.transpose(c_columns[:], c_rows[:])
         nc.vector.tensor_copy(
@@ -47,7 +53,11 @@ def tile_gather_matmul_kernel(tc, table, w, c, offs, out):
 
         def product(bank, b, t, first, last):
             picked = nodes[:].indirect(offsets[:, t * PIECE_COLUMNS : (t + 1) * PIECE_COLUMNS])
-            nc.tensor.matmul(bank[:], weights[t][:, b * P : (b + 1) * P], picked, start=first, stop=last)
+            if t == 0:
+                block_weights = first_weights[:, b * P : (b + 1) * P]
+            else:
+                block_weights = later_weights[b * P // PAIR][:, t - 1, b * P % PAIR : b * P % PAIR + P]
+            nc.tensor.matmul(bank[:], block_weights, picked, start=first, stop=last)
 
         sums = [banks.tile([P, PICKED], F32, name=f"sum{b}") for b in range(BLOCKS)]
         for b in range(BLOCKS):
@@ -55,9 +65,8 @@ def tile_gather_matmul_kernel(tc, table, w, c, offs, out):
 
         out_blocks = out.rearrange("(b p) v -> b p v", p=P)
         for b in range(BLOCKS):
-            second, third = (1, 2) if b < BLOCKS // 2 else (2, 1)
-            product(sums[b], b, second, first=False, last=False)
-            product(sums[b], b, third, first=False, last=True)
+            product(sums[b], b, 1, first=False, last=False)
+            product(sums[b], b, 2, first=False, last=True)
             for queue, columns in ((nc.sync, slice(0, PICKED // 2)), (nc.scalar, slice(PICKED // 2, PICKED))):
                 nc.vector.tensor_tensor(
                     scaled[:, b, columns], sums[b][:, columns], factor[:, columns], mybir.AluOpType.mult

@@ -34,13 +34,13 @@ def tile_gather_matmul_kernel(tc, table, w, c, offs, out):
         scaled = held.tile([P, BLOCKS, PICKED], F32, name="scaled")
 
         nc.vector.memset(c_rows[:], 0.0)
+        nc.sync.dma_start(nodes[:], table)
         nc.sync.dma_start(offsets[:], offs)
         nc.sync.dma_start(first_weights[:, 0:P], w[0][:, 0:P])
-        nc.scalar.dma_start(nodes[:], table)
-        nc.scalar.dma_start(c_rows[0:P:SQUARE, :], c.rearrange("o v -> (o v)").partition_broadcast(P // SQUARE))
-        nc.scalar.dma_start(first_weights[:, P:FEATURES], w[0][:, P:FEATURES])
+        nc.sync.dma_start(c_rows[0:P:SQUARE, :], c.rearrange("o v -> (o v)").partition_broadcast(P // SQUARE))
+        nc.sync.dma_start(first_weights[:, P:FEATURES], w[0][:, P:FEATURES])
         for h in range(FEATURES // PAIR):
-            nc.scalar.dma_start(
+            nc.sync.dma_start(
                 later_weights[h][:], w[1:RELATIONS, :, h * PAIR : (h + 1) * PAIR].rearrange("t k m -> k t m")
             )
 

import concourse.mybir as mybir

BF16, F32, U16 = mybir.dt.bfloat16, mybir.dt.float32, mybir.dt.uint16

P = 128
NODES = 1024
RELATIONS = 3
PICKED = 256
FEATURES = 512
BLOCKS = FEATURES // P
PIECE_COLUMNS = PICKED // 16
PAIR = 2 * P
SQUARE = 32

FLOPS = 2 * RELATIONS * P * FEATURES * PICKED


def tile_gather_matmul_kernel(tc, table, w, c, offs, out):
    nc = tc.nc
    with (
        tc.tile_pool(name="held", bufs=1) as held,
        tc.psum_pool(name="banks", bufs=1) as banks,
    ):
        offsets = held.tile([P, RELATIONS * PIECE_COLUMNS], U16, name="offsets")
        nodes = held.tile([P, NODES], BF16, name="nodes")
        first_weights = held.tile([P, FEATURES], BF16, name="first_weights")
        later_weights = [
            held.tile([P, RELATIONS - 1, PAIR], BF16, name=f"later_weights{h}") for h in range(FEATURES // PAIR)
        ]
        c_rows = held.tile([P, PICKED], F32, name="c_rows", align_bytes=64)
        c_columns = held.tile([P, PICKED], F32, name="c_columns", align_bytes=64)
        c_repeated = held.tile([P, PICKED], F32, name="c_repeated", align_bytes=64)
        factor = held.tile([P, PICKED], F32, name="factor", align_bytes=64)
        scaled = held.tile([P, BLOCKS, PICKED], F32, name="scaled")

        nc.vector.memset(c_rows[:], 0.0)
        nc.sync.dma_start(nodes[:], table)
        nc.sync.dma_start(offsets[:], offs)
        nc.sync.dma_start(first_weights[:, 0:P], w[0][:, 0:P])
        nc.sync.dma_start(c_rows[0:P:SQUARE, :], c.rearrange("o v -> (o v)").partition_broadcast(P // SQUARE))
        nc.sync.dma_start(first_weights[:, P:FEATURES], w[0][:, P:FEATURES])
        for h in range(FEATURES // PAIR):
            nc.sync.dma_start(
                later_weights[h][:], w[1:RELATIONS, :, h * PAIR : (h + 1) * PAIR].rearrange("t k m -> k t m")
            )

        nc.vector.transpose(c_columns[:], c_rows[:])
        nc.vector.tensor_copy(
            c_repeated[:].rearrange("p (s q) -> p s q", q=SQUARE),
            c_columns[:].rearrange("p (s q) -> p s q", q=SQUARE)[:, :, 0:1].to_broadcast([P, PICKED // SQUARE, SQUARE]),
        )
        nc.vector.transpose(factor[:], c_repeated[:])

        def product(bank, b, t, first, last):
            picked = nodes[:].indirect(offsets[:, t * PIECE_COLUMNS : (t + 1) * PIECE_COLUMNS])
            if t == 0:
                block_weights = first_weights[:, b * P : (b + 1) * P]
            else:
                block_weights = later_weights[b * P // PAIR][:, t - 1, b * P % PAIR : b * P % PAIR + P]
            nc.tensor.matmul(bank[:], block_weights, picked, start=first, stop=last)

        sums = [banks.tile([P, PICKED], F32, name=f"sum{b}") for b in range(BLOCKS)]
        for b in range(BLOCKS):
            product(sums[b], b, 0, first=True, last=False)

        out_blocks = out.rearrange("(b p) v -> b p v", p=P)
        for b in range(BLOCKS):
            product(sums[b], b, 1, first=False, last=False)
            product(sums[b], b, 2, first=False, last=True)
            for queue, columns in ((nc.sync, slice(0, PICKED // 2)), (nc.scalar, slice(PICKED // 2, PICKED))):
                nc.vector.tensor_tensor(
                    scaled[:, b, columns], sums[b][:, columns], factor[:, columns], mybir.AluOpType.mult
                )
                queue.dma_start(out_blocks[b][:, columns], scaled[:, b, columns])
